import numpy as np
import ml_dtypes

BF16 = ml_dtypes.bfloat16


def bf(x):
    return np.asarray(x, np.float32).astype(BF16)


def f32(x):
    return np.asarray(x, np.float32)


def f64(x):
    return np.asarray(x).astype(np.float64)


def striped(idx):
    return np.tile(idx.reshape(-1, 16).T, (8, 1))


def rows(idx, k):
    return np.tile(idx, (k, 1))


def look(tab, idx):
    return np.take_along_axis(f64(tab), rows(idx, len(tab)), axis=1)


K, S, V, N, M = 128, 2048, 1536, 1536, 512


def setup_inputs():
    return {"tab": f32(np.random.standard_normal((K, S))), "w": bf(np.random.standard_normal((K, M)) / np.sqrt(K)), "b": f32(0.5 * np.random.standard_normal((M, 1))), "offs": striped(np.random.randint(0, S, N))}


def reference(tab, w, b, offs):
    idx = offs[:16].T.reshape(-1)
    t = look(tab, idx)
    x = (t >= 0.25) * 0.5
    y = f64(w).T @ x
    return y + f64(b)

@@ -1,0 +1,51 @@
+import concourse.mybir as mybir
+
+P = 128
+S = 2048
+N = 1536
+M = 512
+C = M // P
+PIECE = 512
+THRESHOLD, HIGH = 0.25, 0.5
+
+FLOPS = 2 * P * M * N
+F32, BF16, U16 = mybir.dt.float32, mybir.dt.bfloat16, mybir.dt.uint16
+ge, mult, add = mybir.AluOpType.is_ge, mybir.AluOpType.mult, mybir.AluOpType.add
+identity = mybir.ActivationFunctionType.Identity
+
+
+def tile_lookup_deq_step_bias_kernel(tc, tab, w, b, offs, out):
+    nc = tc.nc
+    b_by_partition = b.rearrange("(p c) one -> p (c one)", c=C)
+    out_by_partition = out.rearrange("(p c) j -> p c j", c=C)
+    with (
+        tc.tile_pool(name="held", bufs=1) as held,
+        tc.tile_pool(name="step", bufs=3) as step,
+        tc.tile_pool(name="results", bufs=N // PIECE * C) as results,
+        tc.psum_pool(name="psum", bufs=8) as psum,
+    ):
+        offsets = held.tile([P, N // 16], U16, name="offsets")
+        table = held.tile([P, S], F32, name="table")
+        weights = held.tile([P, M], BF16, name="weights")
+        bias = held.tile([P, C], F32, name="bias")
+        nc.sync.dma_start(offsets[:], offs)
+        nc.sync.dma_start(table[:, : S // 2], tab[:, : S // 2])
+        nc.scalar.dma_start(table[:, S // 2 :], tab[:, S // 2 :])
+        nc.scalar.dma_start(weights[:], w)
+        nc.gpsimd.dma_start(bias[:], b_by_partition)
+
+        for k in range(N // PIECE):
+            x = step.tile([P, PIECE], F32, name="x")
+            piece = offsets[:, k * PIECE // 16 : (k + 1) * PIECE // 16]
+            nc.vector.tensor_scalar(x[:], table[:].indirect(piece), THRESHOLD, HIGH, ge, mult)
+            x_narrow = step.tile([P, PIECE], BF16, name="x_narrow")
+            nc.scalar.copy(x_narrow[:], x[:])
+            for c in range(C):
+                product = psum.tile([P, PIECE], F32, name="product")
+                nc.tensor.matmul(product[:], weights[:, c::C], x_narrow[:], start=True, stop=True)
+                result = results.tile([P, PIECE], F32, name="result")
+                if k == 0 or c % 2 == 0:
+                    nc.scalar.activation(result[:], product[:], identity, bias=bias[:, c : c + 1])
+                else:
+                    nc.vector.tensor_scalar(result[:], product[:], bias[:, c : c + 1], None, add)
+                nc.sync.dma_start(out_by_partition[:, c, k * PIECE : (k + 1) * PIECE], result[:])

@@ -38,11 +38,10 @@ def tile_lookup_deq_step_bias_kernel(tc, tab, w, b, offs, out):
             x = step.tile([P, PIECE], F32, name="x")
             piece = offsets[:, k * PIECE // 16 : (k + 1) * PIECE // 16]
             nc.vector.tensor_scalar(x[:], table[:].indirect(piece), THRESHOLD, HIGH, ge, mult)
-            x_narrow = step.tile([P, PIECE], BF16, name="x_narrow")
-            nc.scalar.copy(x_narrow[:], x[:])
+            x_narrow = x[:].bitcast(BF16)[:, 1::2]
             for c in range(C):
                 product = psum.tile([P, PIECE], F32, name="product")
-                nc.tensor.matmul(product[:], weights[:, c::C], x_narrow[:], start=True, stop=True)
+                nc.tensor.matmul(product[:], weights[:, c::C], x_narrow, start=True, stop=True)
                 result = results.tile([P, PIECE], F32, name="result")
                 if k == 0 or c % 2 == 0:
                     nc.scalar.activation(result[:], product[:], identity, bias=bias[:, c : c + 1])

@@ -5,7 +5,7 @@ S = 2048
 N = 1536
 M = 512
 C = M // P
-PIECE = 512
+BANK = 512
 THRESHOLD, HIGH = 0.25, 0.5
 
 FLOPS = 2 * P * M * N
@@ -18,10 +18,11 @@ def tile_lookup_deq_step_bias_kernel(tc, tab, w, b, offs, out):
     nc = tc.nc
     b_by_partition = b.rearrange("(p c) one -> p (c one)", c=C)
     out_by_partition = out.rearrange("(p c) j -> p c j", c=C)
+    widths = [BANK // 2] + [BANK] * (N // BANK - 1) + [BANK // 2]
     with (
         tc.tile_pool(name="held", bufs=1) as held,
-        tc.tile_pool(name="step", bufs=3) as step,
-        tc.tile_pool(name="results", bufs=N // PIECE * C) as results,
+        tc.tile_pool(name="step", bufs=len(widths)) as step,
+        tc.tile_pool(name="results", bufs=len(widths) * C) as results,
         tc.psum_pool(name="psum", bufs=8) as psum,
     ):
         offsets = held.tile([P, N // 16], U16, name="offsets")
@@ -32,19 +33,21 @@ def tile_lookup_deq_step_bias_kernel(tc, tab, w, b, offs, out):
         nc.sync.dma_start(table[:, : S // 2], tab[:, : S // 2])
         nc.scalar.dma_start(table[:, S // 2 :], tab[:, S // 2 :])
         nc.scalar.dma_start(weights[:], w)
-        nc.gpsimd.dma_start(bias[:], b_by_partition)
+        nc.sync.dma_start(bias[:], b_by_partition)
 
-        for k in range(N // PIECE):
-            x = step.tile([P, PIECE], F32, name="x")
-            piece = offsets[:, k * PIECE // 16 : (k + 1) * PIECE // 16]
+        start = 0
+        for k, width in enumerate(widths):
+            x = step.tile([P, width], F32, name="x")
+            piece = offsets[:, start // 16 : (start + width) // 16]
             nc.vector.tensor_scalar(x[:], table[:].indirect(piece), THRESHOLD, HIGH, ge, mult)
             x_narrow = x[:].bitcast(BF16)[:, 1::2]
             for c in range(C):
-                product = psum.tile([P, PIECE], F32, name="product")
+                product = psum.tile([P, width], F32, name="product")
                 nc.tensor.matmul(product[:], weights[:, c::C], x_narrow, start=True, stop=True)
-                result = results.tile([P, PIECE], F32, name="result")
+                result = results.tile([P, width], F32, name="result")
                 if k == 0 or c % 2 == 0:
                     nc.scalar.activation(result[:], product[:], identity, bias=bias[:, c : c + 1])
                 else:
                     nc.vector.tensor_scalar(result[:], product[:], bias[:, c : c + 1], None, add)
-                nc.sync.dma_start(out_by_partition[:, c, k * PIECE : (k + 1) * PIECE], result[:])
+                nc.sync.dma_start(out_by_partition[:, c, start : start + width], result[:])
+            start += width

@@ -30,8 +30,7 @@ def tile_lookup_deq_step_bias_kernel(tc, tab, w, b, offs, out):
         weights = held.tile([P, M], BF16, name="weights")
         bias = held.tile([P, C], F32, name="bias")
         nc.sync.dma_start(offsets[:], offs)
-        nc.sync.dma_start(table[:, : S // 2], tab[:, : S // 2])
-        nc.scalar.dma_start(table[:, S // 2 :], tab[:, S // 2 :])
+        nc.scalar.dma_start(table[:], tab)
         nc.scalar.dma_start(weights[:], w)
         nc.sync.dma_start(bias[:], b_by_partition)
 

import concourse.mybir as mybir

P = 128
S = 2048
N = 1536
M = 512
C = M // P
BANK = 512
THRESHOLD, HIGH = 0.25, 0.5

FLOPS = 2 * P * M * N
F32, BF16, U16 = mybir.dt.float32, mybir.dt.bfloat16, mybir.dt.uint16
ge, mult, add = mybir.AluOpType.is_ge, mybir.AluOpType.mult, mybir.AluOpType.add
identity = mybir.ActivationFunctionType.Identity


def tile_lookup_deq_step_bias_kernel(tc, tab, w, b, offs, out):
    nc = tc.nc
    b_by_partition = b.rearrange("(p c) one -> p (c one)", c=C)
    out_by_partition = out.rearrange("(p c) j -> p c j", c=C)
    widths = [BANK // 2] + [BANK] * (N // BANK - 1) + [BANK // 2]
    with (
        tc.tile_pool(name="held", bufs=1) as held,
        tc.tile_pool(name="step", bufs=len(widths)) as step,
        tc.tile_pool(name="results", bufs=len(widths) * C) as results,
        tc.psum_pool(name="psum", bufs=8) as psum,
    ):
        offsets = held.tile([P, N // 16], U16, name="offsets")
        table = held.tile([P, S], F32, name="table")
        weights = held.tile([P, M], BF16, name="weights")
        bias = held.tile([P, C], F32, name="bias")
        nc.sync.dma_start(offsets[:], offs)
        nc.scalar.dma_start(table[:], tab)
        nc.scalar.dma_start(weights[:], w)
        nc.sync.dma_start(bias[:], b_by_partition)

        start = 0
        for k, width in enumerate(widths):
            x = step.tile([P, width], F32, name="x")
            piece = offsets[:, start // 16 : (start + width) // 16]
            nc.vector.tensor_scalar(x[:], table[:].indirect(piece), THRESHOLD, HIGH, ge, mult)
            x_narrow = x[:].bitcast(BF16)[:, 1::2]
            for c in range(C):
                product = psum.tile([P, width], F32, name="product")
                nc.tensor.matmul(product[:], weights[:, c::C], x_narrow, start=True, stop=True)
                result = results.tile([P, width], F32, name="result")
                if k == 0 or c % 2 == 0:
                    nc.scalar.activation(result[:], product[:], identity, bias=bias[:, c : c + 1])
                else:
                    nc.vector.tensor_scalar(result[:], product[:], bias[:, c : c + 1], None, add)
                nc.sync.dma_start(out_by_partition[:, c, start : start + width], result[:])
            start += width
